import numpy as np
import ml_dtypes


def mxq(x, axis, fmt="e4m3"):
    dtype, down = {"e4m3": (ml_dtypes.float8_e4m3fn, 7), "e5m2": (ml_dtypes.float8_e5m2, 14)}[fmt]
    v = np.moveaxis(np.asarray(x, np.float32).astype(ml_dtypes.bfloat16).astype(np.float64), axis, -1)
    blocks = v.reshape(v.shape[:-1] + (-1, 32))
    amax = np.abs(blocks).max(-1, keepdims=True)
    byte = np.maximum(np.where(amax > 0, np.frexp(amax)[1] - 1 + 127, 0) - down, 1)
    scale = np.exp2(byte - 127.0)
    codes = (blocks / scale).astype(np.float32).astype(dtype).astype(np.float64)
    return np.moveaxis((codes * scale).reshape(v.shape), -1, axis)


WIDE = False


def mx_kscale(k):
    if not WIDE:
        return np.ones(k)
    levels = np.array([30, -30])
    if k % 512:
        return np.exp2(np.random.permutation(np.resize(levels, k // 32))).repeat(32)
    a = np.empty((k // 512, 16))
    for p in range(k // 512):
        a[p, :8] = np.random.permutation(np.resize(levels, 8))
        for g in range(8):
            far = levels[np.abs(levels - a[p, g]) >= 10]
            a[p, g + 8] = far[np.random.randint(len(far))]
    return np.exp2(a.ravel()).repeat(32)


BF16 = ml_dtypes.bfloat16


def bf(x):
    return np.asarray(x, np.float32).astype(BF16)


def f64(x):
    return np.asarray(x).astype(np.float64)


E2M1 = np.array([0.0, 0.5, 1.0, 1.5, 2.0, 3.0, 4.0, 6.0, -0.0, -0.5, -1.0, -1.5, -2.0, -3.0, -4.0, -6.0])


def pack_weight(w, fmt):
    k, n = w.shape
    w = f64(bf(w)).reshape(k // 32, 32, n)
    amax = np.abs(w).max(1)
    if fmt in ("e4m3", "e5m2"):
        byte = np.frexp(amax)[1] - 1 + 127 - (7 if fmt == "e4m3" else 14)
    else:
        mant, ex = np.frexp(amax / 6.0)
        byte = np.where(mant > 0.5, ex, ex - 1) + 127
    byte = np.clip(np.where(amax > 0, byte, 1), 1, 254)
    scaled = (w * np.exp2(127.0 - byte)[:, None, :]).reshape(k, n).astype(np.float32)
    by_word = np.ascontiguousarray(scaled.reshape(k // 512, 128, 4, n).transpose(0, 1, 3, 2))
    if fmt in ("e4m3", "e5m2"):
        words = by_word.astype(ml_dtypes.float8_e4m3fn if fmt == "e4m3" else ml_dtypes.float8_e5m2).view(np.uint8)
    else:
        c = by_word.astype(ml_dtypes.float4_e2m1fn).view(np.uint8) & 0xF
        words = c[..., 0::2] | (c[..., 1::2] << 4)
    return np.ascontiguousarray(words), np.ascontiguousarray(byte.astype(np.uint8).reshape(k // 512, 16, n))


def unpack_weight(words, scales, fmt):
    g, p, n, _ = words.shape
    if fmt in ("e4m3", "e5m2"):
        vals = np.ascontiguousarray(words).view(ml_dtypes.float8_e4m3fn if fmt == "e4m3" else ml_dtypes.float8_e5m2).astype(np.float64)
    else:
        nib = np.empty((g, p, n, 4), np.uint8)
        nib[..., 0::2] = words & 0xF
        nib[..., 1::2] = words >> 4
        vals = E2M1[nib]
    vals = vals * np.repeat(np.exp2(scales.astype(np.float64) - 127.0), 8, axis=1)[..., None]
    return vals.transpose(0, 1, 3, 2).reshape(g * 512, n)

def planes(Y):
    n, m = Y.shape
    b = f64(bf(Y)).reshape(n // 32, 32, m)
    amax = np.abs(b).max(1)
    byte = np.clip(np.where(amax > 0, np.frexp(amax)[1] - 1 + 127 - 7, 1), 1, 254)
    codes = (b * np.exp2(127.0 - byte)[:, None, :]).reshape(n, m).astype(np.float32).astype(ml_dtypes.float8_e4m3fn).view(np.uint8)
    words = codes.reshape(n // 512, 128, 4, m).transpose(0, 1, 3, 2)
    return np.ascontiguousarray(words), np.ascontiguousarray(byte.astype(np.uint8).reshape(n // 512, 16, m))


M, D = 1024, 1536


def setup_inputs():
    s = mx_kscale(D)
    errors = 0.6 * np.random.standard_t(3, (D, M))
    err_words, err_scales = pack_weight(errors * s[:, None], "e5m2")
    prop = 0.8 * np.random.randn(D, D) / np.sqrt(D)
    return {
        "err_words": err_words,
        "err_scales": err_scales,
        "prop": bf(prop / s[:, None]),
        "infl": bf(np.exp(0.3 * np.random.randn(D))),
        "forcing": bf(0.4 * np.random.randn(M, D)),
        "member_scale": bf(np.exp(0.7 * np.random.randn(M))),
    }


def reference(err_words, err_scales, prop, infl, forcing, member_scale):
    E = unpack_weight(err_words, err_scales, "e5m2")
    A = mxq(f64(prop), 0, "e4m3")
    moved = E.T @ A
    grown = moved * f64(infl)[None, :] + f64(forcing)
    y = grown * f64(member_scale)[:, None]
    Y = y.reshape(M, D)
    words, scales = planes(Y)
    return y, words, scales

from contextlib import ExitStack

import concourse.mybir as mybir
from concourse.masks import make_identity

M, D = 1024, 1536
FLOPS = 2 * M * D * D
P = 128
PACK = 4
N = 512
GROUPS = D // N
HALVES = M // N

F32 = mybir.dt.float32
BF16 = mybir.dt.bfloat16
I32 = mybir.dt.int32
U32 = mybir.dt.uint32
U8 = mybir.dt.uint8
E4M3X4 = mybir.dt.float8_e4m3fn_x4
E5M2X4 = mybir.dt.float8_e5m2_x4
MULT = mybir.AluOpType.mult
ADD = mybir.AluOpType.add
COPY = mybir.ActivationFunctionType.Copy


FAST = False
UNITS = [(0,0,512),(1,0,512),(0,512,1024),(1,512,1024),(0,1024,1536),(1,1024,1536)]
A_SLOTS = 4
Y_BUFS = 1
ORDER = [
    ("load_a", (0, 0, 512,)),
    ("esc", (0,)),
    ("esc", (1,)),
    ("esc", (2,)),
    ("esc", (3,)),
    ("load_a", (1, 0, 512,)),
    ("load_e", (0, 0, 1,)),
    ("load_a", (2, 0, 512,)),
    ("load_e", (0, 1, 2,)),
    ("load_e", (0, 2, 3,)),
    ("load_a", (0, 512, 1024,)),
    ("load_e", (1, 0, 3,)),
    ("load_a", (1, 512, 1024,)),
    ("load_a", (2, 512, 1024,)),
    ("load_f", (0, 0, 512,)),
    ("load_f", (1, 0, 512,)),
    ("load_a", (0, 1024, 1536,)),
    ("load_a", (1, 1024, 1536,)),
    ("load_f", (0, 512, 1536,)),
    ("load_a", (2, 1024, 1536,)),
    ("load_f", (1, 512, 1536,)),
    ("cast_infl", ()),
    ("widen_weight", ()),
    ("flip_infl", ()),
    ("flip_weight", (0,)),
    ("group_a", ("V", 0, 0, 320,)),
    ("group_a", ("S", 0, 320, 512,)),
    ("quant_a", (0, 0, 512,)),
    ("take_infl", ()),
    ("multiply", (0, 0, 0,)),
    ("multiply", (0, 128, 0,)),
    ("multiply", (0, 256, 0,)),
    ("multiply", (0, 384, 0,)),
    ("group_a", ("V", 1, 0, 288,)),
    ("group_a", ("S", 1, 288, 512,)),
    ("quant_a", (1, 0, 512,)),
    ("take_weight", (0,)),
    ("multiply", (0, 0, 1,)),
    ("multiply", (0, 128, 1,)),
    ("multiply", (0, 256, 1,)),
    ("multiply", (0, 384, 1,)),
    ("group_a", ("V", 2, 0, 320,)),
    ("group_a", ("S", 2, 320, 512,)),
    ("quant_a", (2, 0, 512,)),
    ("multiply", (0, 0, 2,)),
    ("multiply", (0, 128, 2,)),
    ("multiply", (0, 256, 2,)),
    ("multiply", (0, 384, 2,)),
    ("group_a", ("V", 0, 512, 1024,)),
    ("quant_a", (0, 512, 1024,)),
    ("inflate", (0, 0,)),
    ("inflate", (0, 128,)),
    ("inflate", (0, 256,)),
    ("inflate", (0, 384,)),
    ("multiply", (1, 0, 0,)),
    ("multiply", (1, 0, 1,)),
    ("multiply", (1, 0, 2,)),
    ("multiply", (1, 128, 0,)),
    ("multiply", (1, 128, 1,)),
    ("multiply", (1, 128, 2,)),
    ("multiply", (1, 256, 0,)),
    ("multiply", (1, 256, 1,)),
    ("multiply", (1, 256, 2,)),
    ("multiply", (1, 384, 0,)),
    ("multiply", (1, 384, 1,)),
    ("multiply", (1, 384, 2,)),
    ("inflate", (1, 0,)),
    ("group_a", ("V", 1, 512, 992,)),
    ("group_a", ("S", 1, 992, 1024,)),
    ("inflate", (1, 128,)),
    ("group_a", ("V", 2, 512, 768,)),
    ("group_a", ("S", 2, 768, 1024,)),
    ("quant_a", (1, 512, 1024,)),
    ("inflate", (1, 256,)),
    ("weigh_f", ("V", 0, 0, 0, 512,)),
    ("quant_a", (2, 512, 1024,)),
    ("weigh_f", ("S", 0, 1, 0, 512,)),
    ("weigh_f", ("V", 0, 2, 0, 512,)),
    ("weigh_f", ("S", 0, 3, 0, 512,)),
    ("inflate", (1, 384,)),
    ("turn_run", (0, 0, 0, 512,)),
    ("turn_run", (0, 1, 0, 512,)),
    ("turn_run", (0, 2, 0, 512,)),
    ("turn_run", (0, 3, 0, 512,)),
    ("multiply", (0, 512, 0,)),
    ("multiply", (0, 512, 1,)),
    ("multiply", (0, 512, 2,)),
    ("multiply", (0, 640, 0,)),
    ("multiply", (0, 640, 1,)),
    ("multiply", (0, 640, 2,)),
    ("multiply", (0, 768, 0,)),
    ("multiply", (0, 768, 1,)),
    ("multiply", (0, 768, 2,)),
    ("multiply", (0, 896, 0,)),
    ("multiply", (0, 896, 1,)),
    ("multiply", (0, 896, 2,)),
    ("finish", (0, 0, 0, 512,)),
    ("finish", (0, 1, 0, 512,)),
    ("finish", (0, 2, 0, 512,)),
    ("finish", (0, 3, 0, 512,)),
    ("store_y", ("Y", 0, 0, 4, 0, 512,)),
    ("weigh_f", ("V", 1, 0, 0, 512,)),
    ("weigh_f", ("S", 1, 1, 0, 512,)),
    ("weigh_f", ("S", 1, 2, 0, 512,)),
    ("weigh_f", ("S", 1, 3, 0, 512,)),
    ("group_y", ("G", 0, 0, 512,)),
    ("turn_run", (1, 0, 0, 512,)),
    ("turn_run", (1, 1, 0, 512,)),
    ("turn_run", (1, 2, 0, 512,)),
    ("turn_run", (1, 3, 0, 512,)),
    ("inflate_v", (0, 512,)),
    ("inflate_v", (0, 640,)),
    ("inflate_v", (0, 768,)),
    ("inflate_v", (0, 896,)),
    ("multiply", (1, 512, 0,)),
    ("multiply", (1, 512, 1,)),
    ("multiply", (1, 512, 2,)),
    ("multiply", (1, 640, 0,)),
    ("multiply", (1, 640, 1,)),
    ("multiply", (1, 640, 2,)),
    ("multiply", (1, 768, 0,)),
    ("multiply", (1, 768, 1,)),
    ("multiply", (1, 768, 2,)),
    ("multiply", (1, 896, 0,)),
    ("multiply", (1, 896, 1,)),
    ("multiply", (1, 896, 2,)),
    ("finish", (1, 0, 0, 512,)),
    ("finish", (1, 1, 0, 512,)),
    ("finish", (1, 2, 0, 512,)),
    ("finish", (1, 3, 0, 512,)),
    ("store_y", ("Y", 1, 0, 4, 0, 512,)),
    ("group_a", ("S", 0, 1024, 1536,)),
    ("group_a", ("S", 1, 1024, 1536,)),
    ("group_a", ("V", 2, 1024, 1248,)),
    ("group_a", ("S", 2, 1248, 1536,)),
    ("quant_a", (0, 1024, 1536,)),
    ("quant_a", (1, 1024, 1536,)),
    ("quant_a", (2, 1024, 1536,)),
    ("quant_y", (0, 0, 512,)),
    ("store_codes", ("Y", 0, 0, 512,)),
    ("turn_run", (0, 0, 512, 1024,)),
    ("turn_run", (0, 1, 512, 1024,)),
    ("turn_run", (0, 2, 512, 1024,)),
    ("turn_run", (0, 3, 512, 1024,)),
    ("group_y", ("G", 1, 0, 320,)),
    ("inflate", (1, 512,)),
    ("inflate", (1, 640,)),
    ("inflate", (1, 768,)),
    ("inflate", (1, 896,)),
    ("group_y", ("S", 1, 320, 512,)),
    ("multiply", (0, 1024, 0,)),
    ("multiply", (0, 1024, 1,)),
    ("multiply", (0, 1024, 2,)),
    ("multiply", (0, 1152, 0,)),
    ("multiply", (0, 1152, 1,)),
    ("multiply", (0, 1152, 2,)),
    ("multiply", (0, 1280, 0,)),
    ("multiply", (0, 1280, 1,)),
    ("multiply", (0, 1280, 2,)),
    ("multiply", (0, 1408, 0,)),
    ("multiply", (0, 1408, 1,)),
    ("multiply", (0, 1408, 2,)),
    ("finish_v", (0, 0, 512, 1024,)),
    ("finish_v", (0, 1, 512, 1024,)),
    ("store_y", ("Y", 0, 0, 2, 512, 1024,)),
    ("finish_v", (0, 2, 512, 1024,)),
    ("finish_v", (0, 3, 512, 1024,)),
    ("store_y", ("Y", 0, 2, 4, 512, 1024,)),
    ("inflate_v", (0, 1024,)),
    ("quant_y", (1, 0, 512,)),
    ("store_codes", ("Y", 1, 0, 512,)),
    ("weigh_f", ("S", 1, 0, 512, 1536,)),
    ("weigh_f", ("S", 1, 1, 512, 1536,)),
    ("weigh_f", ("S", 1, 2, 512, 1536,)),
    ("weigh_f", ("S", 1, 3, 512, 1536,)),
    ("group_y", ("G", 0, 512, 1024,)),
    ("turn_run", (1, 0, 512, 1024,)),
    ("turn_run", (1, 1, 512, 1024,)),
    ("turn_run", (1, 2, 512, 1024,)),
    ("turn_run", (1, 3, 512, 1024,)),
    ("inflate_v", (0, 1152,)),
    ("inflate_v", (0, 1280,)),
    ("inflate_v", (0, 1408,)),
    ("multiply", (1, 1024, 0,)),
    ("multiply", (1, 1024, 1,)),
    ("multiply", (1, 1024, 2,)),
    ("multiply", (1, 1152, 0,)),
    ("multiply", (1, 1152, 1,)),
    ("multiply", (1, 1152, 2,)),
    ("multiply", (1, 1280, 0,)),
    ("multiply", (1, 1280, 1,)),
    ("multiply", (1, 1280, 2,)),
    ("multiply", (1, 1408, 0,)),
    ("multiply", (1, 1408, 1,)),
    ("multiply", (1, 1408, 2,)),
    ("finish", (1, 0, 512, 1024,)),
    ("finish", (1, 1, 512, 1024,)),
    ("store_y", ("Y", 1, 0, 2, 512, 1024,)),
    ("finish", (1, 2, 512, 1024,)),
    ("finish", (1, 3, 512, 1024,)),
    ("store_y", ("Y", 1, 2, 4, 512, 1024,)),
    ("quant_y", (0, 512, 1024,)),
    ("store_codes", ("Y", 0, 512, 1024,)),
    ("group_y", ("G", 1, 512, 832,)),
    ("inflate", (1, 1024,)),
    ("inflate", (1, 1152,)),
    ("inflate", (1, 1280,)),
    ("group_y", ("S", 1, 832, 1024,)),
    ("inflate", (1, 1408,)),
    ("turn_run", (0, 0, 1024, 1536,)),
    ("turn_run", (0, 1, 1024, 1536,)),
    ("turn_run", (0, 2, 1024, 1536,)),
    ("turn_run", (0, 3, 1024, 1536,)),
    ("finish_v", (0, 0, 1024, 1536,)),
    ("finish_v", (0, 1, 1024, 1536,)),
    ("store_y", ("Y", 0, 0, 2, 1024, 1536,)),
    ("finish_v", (0, 2, 1024, 1536,)),
    ("finish_v", (0, 3, 1024, 1536,)),
    ("store_y", ("Y", 0, 2, 4, 1024, 1536,)),
    ("turn_run", (1, 0, 1024, 1536,)),
    ("turn_run", (1, 1, 1024, 1536,)),
    ("turn_run", (1, 2, 1024, 1536,)),
    ("turn_run", (1, 3, 1024, 1536,)),
    ("quant_y", (1, 512, 1024,)),
    ("store_codes", ("Y", 1, 512, 1024,)),
    ("store_scales", ("Y", 0, 0, 2, 0, 1024,)),
    ("store_scales", ("Y", 1, 0, 2, 0, 1024,)),
    ("store_scales", ("Y", 2, 0, 2, 0, 1024,)),
    ("store_scales", ("Y", 3, 0, 2, 0, 1024,)),
    ("group_y", ("G", 0, 1024, 1344,)),
    ("group_y", ("S", 0, 1344, 1536,)),
    ("finish", (1, 0, 1024, 1536,)),
    ("store_y", ("Y", 1, 0, 1, 1024, 1536,)),
    ("finish", (1, 1, 1024, 1536,)),
    ("store_y", ("Y", 1, 1, 2, 1024, 1536,)),
    ("finish", (1, 2, 1024, 1536,)),
    ("store_y", ("Y", 1, 2, 3, 1024, 1536,)),
    ("finish", (1, 3, 1024, 1536,)),
    ("store_y", ("Y", 1, 3, 4, 1024, 1536,)),
    ("quant_y", (0, 1024, 1536,)),
    ("store_codes", ("Y", 0, 1024, 1536,)),
    ("group_y", ("V", 1, 1024, 1280,)),
    ("group_y", ("V", 1, 1280, 1344,)),
    ("group_y", ("S", 1, 1344, 1536,)),
    ("quant_y", (1, 1024, 1280,)),
    ("quant_y", (1, 1280, 1536,)),
    ("store_codes", ("Y", 1, 1024, 1536,)),
    ("store_scales", ("Y", 0, 0, 2, 1024, 1536,)),
    ("store_scales", ("S", 1, 0, 2, 1024, 1536,)),
    ("store_scales", ("Y", 2, 0, 2, 1024, 1536,)),
    ("store_scales", ("S", 3, 0, 2, 1024, 1536,)),
]


def block_of(c):
    return c // N * N


def unit_of(h, c):
    return max(b for hh, b, e in UNITS if hh == h and b <= c)


def unit_no(h, b):
    return [(hh, bb) for hh, bb, e in UNITS].index((h, b))


def issue(s):
    s["setup"]()
    for name, args in ORDER:
        s[name](*args)


def tile_lim_error_samples_step_k2_kernel(
    tc, err_words, err_scales, prop, infl, forcing, member_scale, out_0, out_1, out_2
):
    nc = tc.nc
    with ExitStack() as ctx:
        keep = ctx.enter_context(tc.tile_pool(name="keep", bufs=1))
        ring = ctx.enter_context(tc.tile_pool(name="ring", bufs=2))
        psum = ctx.enter_context(tc.psum_pool(name="psum", bufs=1))
        ctx.enter_context(tc.manual_schedule())

        zero = keep.tile([P, 1], F32, name="zero")
        ident = keep.tile([P, P], F32, name="ident")
        infl_rows = keep.tile([P, P], BF16, name="infl_rows")
        infl_wide = keep.tile([P, P], F32, name="infl_wide")
        infl_cols = keep.tile([P, D // P], F32, name="infl_cols")
        weight = keep.tile([P, HALVES, PACK], BF16, name="weight")
        weight32 = keep.tile([P, HALVES, PACK], F32, name="weight32")
        weight_rows = keep.tile([P, HALVES, N], F32, name="weight_rows")
        e_scales = keep.tile([P, GROUPS, M], U8, name="e_scales", align_bytes=64)
        e_codes = [
            keep.tile([P, GROUPS, N], U32, name="e_codes%d" % h, align_bytes=64) for h in range(HALVES)
        ]
        a_codes = keep.tile([P, GROUPS, D], U32, name="a_codes", align_bytes=64)
        a_scales = keep.tile([P, GROUPS, D], U8, name="a_scales", align_bytes=64)
        a_raw = keep.tile([P, GROUPS, PACK, D], BF16, name="a_raw", align_bytes=64)
        a_grouped = keep.tile([P, A_SLOTS, N, PACK], BF16, name="a_grouped", align_bytes=64)
        f_raw = keep.tile([P, HALVES, PACK, D], BF16, name="f_raw", align_bytes=64)
        y = keep.tile([P, HALVES, PACK, D], F32, name="y", align_bytes=64)
        y_grouped = keep.tile([P, Y_BUFS, N, PACK], BF16, name="y_grouped", align_bytes=64)
        y_codes = keep.tile([P, HALVES, D], U32, name="y_codes", align_bytes=64)
        y_scales = keep.tile([P, HALVES, D], U8, name="y_scales", align_bytes=64)
        sums = {}
        scaled = {}
        turned = {}

        def interleave(engine, dst, src):
            if FAST and engine != "G":
                dst = dst.rearrange("p (c i) t -> p c t i", i=4)
                src = src.rearrange("p t (c i) -> p c t i", i=4)
            else:
                src = src.rearrange("p t c -> p c t")
            if engine == "V":
                nc.vector.tensor_copy(out=dst, in_=src)
            elif engine == "S":
                nc.scalar.copy(out=dst, in_=src)
            else:
                nc.gpsimd.tensor_scalar(dst, src, 1.0, 1.0, MULT, MULT)

        def setup():
            nc.vector.memset(zero[:], 0.0)
            nc.vector.memset(e_scales[:].rearrange("p g n -> p (g n)").bitcast(I32), 0)
            nc.vector.memset(ident[:], 0.0)
            make_identity(nc, ident[:], nomemset=True)
            nc.scalar.dma_start(out=infl_rows[0 : D // P, :], in_=infl.rearrange("(c p) -> c p", p=P))
            nc.scalar.dma_start(
                out=weight[:], in_=member_scale.rearrange("(h p t) -> p h t", h=HALVES, t=PACK)
            )
            nc.scalar.activation(out=infl_wide[:], in_=zero[:].to_broadcast([P, P]), func=COPY)

        def cast_infl():
            nc.scalar.activation(out=infl_wide[0 : D // P, :], in_=infl_rows[0 : D // P, :], func=COPY)

        def widen_weight():
            nc.scalar.copy(out=weight32[:], in_=weight[:])

        def flip_infl():
            turned["infl"] = psum.tile([P, N], F32, name="turned0")
            nc.tensor.transpose(turned["infl"][:, 0:P], infl_wide[:], ident[:])

        def take_infl():
            nc.scalar.copy(out=infl_cols[:], in_=turned["infl"][:, 0 : D // P])

        def flip_weight(h):
            turned["weight", h] = psum.tile([P, N], F32, name="turned%d" % (1 + h))
            for t in range(PACK):
                nc.tensor.transpose(
                    turned["weight", h][:, P * t : P * (t + 1)],
                    weight32[:, h, t : t + 1].to_broadcast([P, P]),
                    ident[:],
                )

        def take_weight(h):
            nc.scalar.copy(out=weight_rows[:, h, :], in_=turned["weight", h][:])

        def inflate_v(h, c):
            scaled[h, c] = ring.tile([P, PACK, P], F32, name="scaled%d" % (c // P % 4))
            nc.vector.scalar_tensor_tensor(
                out=scaled[h, c][:],
                in0=sums[h, c][:].rearrange("j (p t) -> j t p", t=PACK),
                scalar=infl_cols[:, c // P : c // P + 1],
                in1=weight_rows[:, h, :].rearrange("j (t p) -> j t p", t=PACK),
                op0=MULT,
                op1=MULT,
            )

        def finish_v(h, t, c0, c1):
            nc.vector.scalar_tensor_tensor(
                out=y[:, h, t, c0:c1],
                in0=f_raw[:, h, t, c0:c1],
                scalar=weight[:, h, t : t + 1],
                in1=turned[h, t, c0][:, 0 : c1 - c0],
                op0=MULT,
                op1=ADD,
            )

        def load_a(g, c0, c1):
            rows = prop[N * g : N * (g + 1), c0:c1].rearrange("(p t) j -> p t j", t=PACK)
            nc.sync.dma_start(out=a_raw[:, g, :, c0:c1], in_=rows)

        def esc(q):
            nc.sync.dma_start(
                out=e_scales[32 * q : 32 * q + 4, :, :].bitcast(I32),
                in_=err_scales[:, 4 * q : 4 * q + 4, :].rearrange("g r n -> r g n").bitcast(I32),
            )

        def turn_run(h, t, b, e):
            for c in range(b, e, P):
                turn(h, t, c, b)

        def load_e(h, g0, g1):
            words = err_words.rearrange("g p n t -> p g (n t)")
            nc.sync.dma_start(
                out=e_codes[h][:, g0:g1, :].bitcast(I32),
                in_=words[:, g0:g1, PACK * N * h : PACK * N * (h + 1)].bitcast(I32),
            )

        def load_f(h, c0, c1):
            rows = forcing[N * h : N * (h + 1), c0:c1].rearrange("(p t) j -> p t j", t=PACK)
            nc.sync.dma_start(out=f_raw[:, h, :, c0:c1], in_=rows)

        def group_a(engine, g, c0, c1):
            b = block_of(c0)
            interleave(engine, a_grouped[:, (GROUPS * (b // N) + g) % A_SLOTS, c0 - b : c1 - b, :], a_raw[:, g, :, c0:c1])

        def quant_a(g, c0, c1):
            b = block_of(c0)
            nc.vector.quantize_mx(
                out=a_codes[:, g, c0:c1].bitcast(E4M3X4),
                scales=a_scales[:, g, c0:c1],
                in_=a_grouped[:, (GROUPS * (b // N) + g) % A_SLOTS, c0 - b : c1 - b, :].rearrange("p j t -> p (j t)"),
            )

        def multiply(h, c, g):
            if g == 0:
                sums[h, c] = psum.tile([P, N], F32, name="sums%d" % (c // P % 4))
            nc.tensor.matmul_mx(
                out=sums[h, c][:],
                lhsT=a_codes[:, g, c : c + P].bitcast(E4M3X4),
                lhsT_scale=a_scales[:, g, c : c + P],
                rhs=e_codes[h][:, g, :].bitcast(E5M2X4),
                rhs_scale=e_scales[:, g, N * h : N * (h + 1)],
                start=(g == 0),
                stop=(g == GROUPS - 1),
            )

        def inflate(h, c):
            scaled[h, c] = ring.tile([P, PACK, P], F32, name="scaled%d" % (c // P % 4))
            nc.scalar.activation(
                out=scaled[h, c][:],
                in_=sums[h, c][:].rearrange("j (p t) -> j t p", t=PACK),
                func=COPY,
                scale=infl_cols[:, c // P : c // P + 1],
            )

        def turn(h, t, c, c0):
            if c == c0:
                turned[h, t, c0] = psum.tile([P, N], F32, name="turned%d" % t)
            nc.tensor.transpose(
                turned[h, t, c0][:, c - c0 : c - c0 + P], scaled[h, c][:, t, :], ident[:]
            )

        def weigh_f(engine, h, t, c0, c1):
            if engine == "V":
                nc.vector.tensor_scalar(
                    y[:, h, t, c0:c1], f_raw[:, h, t, c0:c1], weight[:, h, t : t + 1], None, MULT
                )
            else:
                nc.scalar.activation(
                    out=y[:, h, t, c0:c1], in_=f_raw[:, h, t, c0:c1], func=COPY, scale=weight32[:, h, t : t + 1]
                )

        def finish(h, t, c0, c1):
            nc.vector.scalar_tensor_tensor(
                out=y[:, h, t, c0:c1],
                in0=turned[h, t, c0][:, 0 : c1 - c0],
                scalar=weight[:, h, t : t + 1],
                in1=y[:, h, t, c0:c1],
                op0=MULT,
                op1=ADD,
            )

        def queue(name):
            return nc.sync if name == "Y" else nc.scalar

        def store_y(q, h, t0, t1, c0, c1):
            rows = out_0[N * h : N * (h + 1), c0:c1].rearrange("(p t) j -> p t j", t=PACK)
            queue(q).dma_start(out=rows[:, t0:t1, :], in_=y[:, h, t0:t1, c0:c1])

        def group_y(engine, h, c0, c1):
            b = unit_of(h, c0)
            interleave(engine, y_grouped[:, unit_no(h, b) % Y_BUFS, c0 - b : c1 - b, :], y[:, h, :, c0:c1])

        def quant_y(h, c0, c1):
            b = unit_of(h, c0)
            nc.vector.quantize_mx(
                out=y_codes[:, h, c0:c1].bitcast(E4M3X4),
                scales=y_scales[:, h, c0:c1],
                in_=y_grouped[:, unit_no(h, b) % Y_BUFS, c0 - b : c1 - b, :].rearrange("p j t -> p (j t)"),
            )

        def store_codes(q, h, c0, c1):
            words = out_1[h].rearrange("p j t -> p (j t)")
            queue(q).dma_start(
                out=words[:, PACK * c0 : PACK * c1].bitcast(I32), in_=y_codes[:, h, c0:c1].bitcast(I32)
            )

        def store_scales(q, quad, h0, h1, c0, c1):
            rows = out_2[h0:h1, 4 * quad : 4 * quad + 4, c0:c1].rearrange("h r j -> r h j")
            queue(q).dma_start(
                out=rows.bitcast(I32), in_=y_scales[32 * quad : 32 * quad + 4, h0:h1, c0:c1].bitcast(I32)
            )

        issue(
            dict(
                setup=setup, cast_infl=cast_infl, widen_weight=widen_weight, flip_infl=flip_infl, take_infl=take_infl, load_a=load_a, esc=esc, flip_weight=flip_weight, take_weight=take_weight, inflate_v=inflate_v, finish_v=finish_v, turn_run=turn_run,
                load_e=load_e, load_f=load_f, group_a=group_a, quant_a=quant_a, multiply=multiply,
                inflate=inflate, turn=turn, weigh_f=weigh_f, finish=finish, store_y=store_y,
                group_y=group_y, quant_y=quant_y, store_codes=store_codes, store_scales=store_scales,
            )
        )
